import numpy as np
import ml_dtypes


def mxq(x, axis, fmt="e4m3"):
    dtype, down = {"e4m3": (ml_dtypes.float8_e4m3fn, 7), "e5m2": (ml_dtypes.float8_e5m2, 14)}[fmt]
    v = np.moveaxis(np.asarray(x, np.float32).astype(ml_dtypes.bfloat16).astype(np.float64), axis, -1)
    blocks = v.reshape(v.shape[:-1] + (-1, 32))
    amax = np.abs(blocks).max(-1, keepdims=True)
    byte = np.maximum(np.where(amax > 0, np.frexp(amax)[1] - 1 + 127, 0) - down, 1)
    scale = np.exp2(byte - 127.0)
    codes = (blocks / scale).astype(np.float32).astype(dtype).astype(np.float64)
    return np.moveaxis((codes * scale).reshape(v.shape), -1, axis)


WIDE = False


def mx_kscale(k):
    if not WIDE:
        return np.ones(k)
    levels = np.array([10, -10, 5, -5, 0])
    if k % 512:
        return np.exp2(np.random.permutation(np.resize(levels, k // 32))).repeat(32)
    a = np.empty((k // 512, 16))
    for p in range(k // 512):
        a[p, :8] = np.random.permutation(np.resize(levels, 8))
        for g in range(8):
            far = levels[np.abs(levels - a[p, g]) >= 10]
            a[p, g + 8] = far[np.random.randint(len(far))]
    return np.exp2(a.ravel()).repeat(32)


def f64(x):
    return np.asarray(x).astype(np.float64)


def striped(idx):
    return np.tile(idx.reshape(-1, 16).T, (8, 1)).astype(np.uint16)


def unstriped(offs):
    return offs[:16].T.reshape(-1).astype(np.int64)


E2M1 = np.array([0.0, 0.5, 1.0, 1.5, 2.0, 3.0, 4.0, 6.0, -0.0, -0.5, -1.0, -1.5, -2.0, -3.0, -4.0, -6.0])


def pack_weight(w, fmt):
    k, n = w.shape
    w = f64(np.asarray(w, np.float32).astype(ml_dtypes.bfloat16)).reshape(k // 32, 32, n)
    amax = np.abs(w).max(1)
    if fmt == "e4m3":
        byte = np.frexp(amax)[1] - 1 + 127 - 7
    else:
        mant, ex = np.frexp(amax / 6.0)
        byte = np.where(mant > 0.5, ex, ex - 1) + 127
    byte = np.clip(np.where(amax > 0, byte, 1), 1, 254)
    scaled = (w * np.exp2(127.0 - byte)[:, None, :]).reshape(k, n).astype(np.float32)
    by_word = np.ascontiguousarray(scaled.reshape(k // 512, 128, 4, n).transpose(0, 1, 3, 2))
    if fmt == "e4m3":
        words = by_word.astype(ml_dtypes.float8_e4m3fn).view(np.uint8)
    else:
        c = by_word.astype(ml_dtypes.float4_e2m1fn).view(np.uint8) & 0xF
        words = (c[..., 0::2] | (c[..., 1::2] << 4)).reshape(k // 512, 128, 2 * n)
    return np.ascontiguousarray(words), np.ascontiguousarray(byte.astype(np.uint8).reshape(k // 512, 16, n))


def unpack_weight(words, scales, fmt):
    g, _, n = scales.shape
    words = np.ascontiguousarray(words).reshape(g, 128, n, -1)
    if fmt == "e4m3":
        vals = words.view(ml_dtypes.float8_e4m3fn).astype(np.float64)
    else:
        nib = np.empty((g, 128, n, 4), np.uint8)
        nib[..., 0::2] = words & 0xF
        nib[..., 1::2] = words >> 4
        vals = E2M1[nib]
    vals = vals * np.repeat(np.exp2(scales.astype(np.float64) - 127.0), 8, axis=1)[..., None]
    return vals.transpose(0, 1, 3, 2).reshape(g * 512, n)


K, T, E, C, N = 384, 1024, 8, 128, 512


def by_expert(wq, xq):
    return np.concatenate([wq[e].T @ xq[:, e * C:(e + 1) * C] for e in range(E)], axis=1)


def setup_inputs():
    n = np.random.standard_normal
    s = mx_kscale(N)[:, None]
    dy = pack_weight(n((N, T)) * s, "e4m3")
    return {
        "dy_words": dy[0],
        "dy_scales": dy[1],
        "w": (n((E + 1, N, K)) / np.sqrt(N) / s[None]).astype(np.float32),
        "gate": np.tile(np.random.uniform(0.2, 1.0, E * C), (K, 1)).astype(np.float32),
        "offs": striped(np.random.permutation(T)[:E * C]),
    }


def reference(dy_words, dy_scales, w, gate, offs):
    idx = unstriped(offs)
    gq = unpack_weight(dy_words, dy_scales, "e4m3")[:, idx]
    wq = mxq(f64(w), 1, "e4m3")
    ds = wq[E].T @ unpack_weight(dy_words, dy_scales, "e4m3")
    dx = f64(gate) * by_expert(wq, gq)
    ds[:, idx] += dx
    return ds

@@ -1,0 +1,172 @@
+from contextlib import ExitStack
+
+import concourse.mybir as mybir
+from concourse.masks import make_identity
+
+K, T, E, C, N = 384, 1024, 8, 128, 512
+FLOPS = 2 * N * K * (E * C + T)
+BYTES = N * T + 16 * T + (E + 1) * N * K * 4 + T * 4 + 128 * 64 * 2 + K * T * 4
+
+F32 = mybir.dt.float32
+BF16 = mybir.dt.bfloat16
+I32 = mybir.dt.int32
+U32 = mybir.dt.uint32
+U16 = mybir.dt.uint16
+U8 = mybir.dt.uint8
+FP8X4 = mybir.dt.float8_e4m3fn_x4
+COPY = mybir.ActivationFunctionType.Copy
+ADD = mybir.AluOpType.add
+
+P = 128
+PACK = 4
+KB = K // P
+HALF = 512
+LIST_COL = 16
+PARTS = ((0, 256), (256, K))
+
+
+def tile_moe_bds_lin_none_kernel(tc, dy_words, dy_scales, w, gate, offs, out):
+    nc = tc.nc
+    with ExitStack() as ctx:
+        keep = ctx.enter_context(tc.tile_pool(name="keep", bufs=1))
+        psum = ctx.enter_context(tc.psum_pool(name="psum", bufs=2))
+
+        offsets = keep.tile([P, T // LIST_COL], U16, name="offsets")
+        token_words = keep.tile([P, T], U32, name="token_words", align_bytes=64)
+        token_scales = keep.tile([P, T], U8, name="token_scales", align_bytes=64)
+        gate_rows = keep.tile([P, C], F32, name="gate_rows")
+        identity = keep.tile([P, P], F32, name="identity")
+        gate_cols = keep.tile([P, E], F32, name="gate_cols")
+
+        nc.vector.memset(token_scales[:].bitcast(I32), 0)
+        nc.gpsimd.memset(gate_rows[:], 0.0)
+        make_identity(nc, identity[:])
+
+        nc.sync.dma_start(offsets[:], offs)
+        nc.sync.dma_start(token_words[:].bitcast(I32), dy_words[0].rearrange("p t d -> p (t d)").bitcast(I32))
+        for r in range(4):
+            nc.sync.dma_start(token_scales[r:P:32, :].bitcast(I32), dy_scales[0][r:16:4, :].bitcast(I32))
+        nc.sync.dma_start(gate_rows[0:E, :], gate[0:1, :].rearrange("o (e c) -> (o e) c", c=C))
+
+        order = [0, E] + list(range(1, E))
+        raw = {}
+        for e in order:
+            raw[e] = keep.tile([P, PACK, K], F32, name="raw%d" % e)
+            nc.sync.dma_start(raw[e][:], w[e].rearrange("(p j) k -> p j k", j=PACK))
+
+        gate_t = psum.tile([P, P], F32, name="gate_t", tag="turned")
+        nc.tensor.transpose(gate_t[:], gate_rows[:], identity[:])
+        nc.scalar.activation(gate_cols[:], gate_t[:, 0:E], COPY)
+
+        slot_words, slot_scales = {}, {}
+
+        def list_cols(s0, s1):
+            return offsets[:, s0 // LIST_COL : s1 // LIST_COL]
+
+        def gather_words(h):
+            slot_words[h] = keep.tile([P, HALF], U32, name="slot_words%d" % h, align_bytes=64)
+            nc.vector.tensor_copy(slot_words[h][:], token_words[:].indirect(list_cols(h * HALF, (h + 1) * HALF)))
+
+        def gather_scales(h, tag):
+            slot_scales[h] = keep.tile([P, HALF], U8, name="slot_scales%d" % h, tag=tag, align_bytes=64)
+            nc.vector.tensor_copy(slot_scales[h][:], token_scales[:].indirect(list_cols(h * HALF, (h + 1) * HALF)))
+
+        grouped, codes, scales, gated, turned = {}, {}, {}, {}, {}
+
+        def cast(e, part, copy):
+            a, b = PARTS[part]
+            grouped[e, part] = keep.tile(
+                [P, b - a, PACK], BF16, name="grouped%d_%d" % (e, part), tag="stage%d_%d" % (e, part), align_bytes=64
+            )
+            copy(
+                grouped[e, part][:].rearrange("p (c i) t -> p c t i", i=4),
+                raw[e][:, :, a:b].rearrange("p t (c i) -> p c t i", i=4),
+            )
+
+        def quantise(e, part):
+            a, b = PARTS[part]
+            if e not in codes:
+                codes[e] = keep.tile([P, K], U32, name="codes%d" % e, align_bytes=64)
+                scales[e] = keep.tile([P, K], U8, name="scales%d" % e, align_bytes=64)
+            nc.vector.quantize_mx(
+                out=codes[e][:, a:b].bitcast(FP8X4),
+                scales=scales[e][:, a:b],
+                in_=grouped[e, part][:].rearrange("p k t -> p (k t)"),
+            )
+
+        dx = keep.tile([P, KB, T], F32, name="dx")
+        ds = keep.tile([P, KB, T], F32, name="ds")
+        windows = [keep.tile([P, T], F32, name="window%d" % kb) for kb in range(KB)]
+
+        def routed(e):
+            h, c0 = divmod(e * C, HALF)
+            sums = psum.tile([P, K], F32, name="sums", tag="sums", bufs=1)
+            for a, b in PARTS:
+                nc.tensor.matmul_mx(
+                    out=sums[:, a:b],
+                    lhsT=slot_words[h][:, c0 : c0 + C].bitcast(FP8X4),
+                    lhsT_scale=slot_scales[h][:, c0 : c0 + C],
+                    rhs=codes[e][:, a:b].bitcast(FP8X4),
+                    rhs_scale=scales[e][:, a:b],
+                    start=True,
+                    stop=True,
+                )
+            tag = "stage%d_0" % (e + 2) if e + 2 < E else "gated%d" % e
+            gated[e] = keep.tile([P, K], F32, name="gated%d" % e, tag=tag, align_bytes=64)
+            nc.scalar.activation(gated[e][:], sums[:], COPY, scale=gate_cols[:, e : e + 1])
+            turned[e] = psum.tile([P, KB, C], F32, name="turned", tag="turned")
+            for kb in range(KB):
+                nc.tensor.transpose(turned[e][:, kb, :], gated[e][:, kb * P : (kb + 1) * P], identity[:])
+
+        def routed_out(e):
+            nc.scalar.copy(dx[:, :, e * C : (e + 1) * C], turned[e][:])
+
+        def shared(e):
+            h, c0 = divmod(e * C, HALF)
+            sums = psum.tile([P, KB, C], F32, name="shared_sums", tag="shared_sums")
+            for kb in range(KB):
+                nc.tensor.matmul_mx(
+                    out=sums[:, kb, :],
+                    lhsT=codes[E][:, kb * P : (kb + 1) * P].bitcast(FP8X4),
+                    lhsT_scale=scales[E][:, kb * P : (kb + 1) * P],
+                    rhs=slot_words[h][:, c0 : c0 + C].bitcast(FP8X4),
+                    rhs_scale=slot_scales[h][:, c0 : c0 + C],
+                    start=True,
+                    stop=True,
+                )
+            nc.scalar.copy(ds[:, :, e * C : (e + 1) * C], sums[:])
+
+        def scatter(e0, e1, kb):
+            s0, s1 = e0 * C, e1 * C
+            nc.vector.tensor_tensor(windows[kb][:].indirect(list_cols(s0, s1)), dx[:, kb, s0:s1], ds[:, kb, s0:s1], ADD)
+            if e1 == E:
+                nc.sync.dma_start(out[kb * P : (kb + 1) * P, :], windows[kb][:])
+
+        gather_words(0)
+        gather_scales(0, "slot_scales0")
+        gather_words(1)
+        for e, copy in ((0, nc.scalar.copy), (E, nc.vector.tensor_copy)):
+            for part in range(2):
+                cast(e, part, copy)
+            for part in range(2):
+                quantise(e, part)
+        gather_scales(1, "stage%d_1" % E)
+        routed(0)
+        for part in range(2):
+            cast(1, part, nc.scalar.copy)
+            quantise(1, part)
+        for e in range(E):
+            if e > 0:
+                routed(e)
+            shared(e)
+            if e + 2 < E:
+                cast(e + 2, 1, nc.scalar.copy)
+            routed_out(e)
+            for kb in range(KB):
+                if e == E - 2 and kb == KB - 1:
+                    continue
+                scatter(e - 1 if (e == E - 1 and kb == KB - 1) else e, e + 1, kb)
+            if e + 2 < E:
+                cast(e + 2, 0, nc.scalar.copy)
+                quantise(e + 2, 1)
+                quantise(e + 2, 0)

@@ -16,6 +16,7 @@ U8 = mybir.dt.uint8
 FP8X4 = mybir.dt.float8_e4m3fn_x4
 COPY = mybir.ActivationFunctionType.Copy
 ADD = mybir.AluOpType.add
+MULT = mybir.AluOpType.mult
 
 P = 128
 PACK = 4
@@ -48,7 +49,7 @@ def tile_moe_bds_lin_none_kernel(tc, dy_words, dy_scales, w, gate, offs, out):
             nc.sync.dma_start(token_scales[r:P:32, :].bitcast(I32), dy_scales[0][r:16:4, :].bitcast(I32))
         nc.sync.dma_start(gate_rows[0:E, :], gate[0:1, :].rearrange("o (e c) -> (o e) c", c=C))
 
-        order = [0, E] + list(range(1, E))
+        order = [E] + list(range(E))
         raw = {}
         for e in order:
             raw[e] = keep.tile([P, PACK, K], F32, name="raw%d" % e)
@@ -57,6 +58,10 @@ def tile_moe_bds_lin_none_kernel(tc, dy_words, dy_scales, w, gate, offs, out):
         gate_t = psum.tile([P, P], F32, name="gate_t", tag="turned")
         nc.tensor.transpose(gate_t[:], gate_rows[:], identity[:])
         nc.scalar.activation(gate_cols[:], gate_t[:, 0:E], COPY)
+        gate_wide = keep.tile([P, 1, C], F32, name="gate_wide", tag="stage2_1", align_bytes=64)
+        gate_spread = psum.tile([P, C], F32, name="gate_spread", tag="turned")
+        nc.tensor.transpose(gate_spread[:], gate_cols[:, 0:1].to_broadcast([P, P]), identity[:])
+        nc.scalar.copy(gate_wide[:, 0, :], gate_spread[:])
 
         slot_words, slot_scales = {}, {}
 
@@ -96,7 +101,7 @@ def tile_moe_bds_lin_none_kernel(tc, dy_words, dy_scales, w, gate, offs, out):
 
         dx = keep.tile([P, KB, T], F32, name="dx")
         ds = keep.tile([P, KB, T], F32, name="ds")
-        windows = [keep.tile([P, T], F32, name="window%d" % kb) for kb in range(KB)]
+        windows = {}
 
         def routed(e):
             h, c0 = divmod(e * C, HALF)
@@ -111,62 +116,78 @@ def tile_moe_bds_lin_none_kernel(tc, dy_words, dy_scales, w, gate, offs, out):
                     start=True,
                     stop=True,
                 )
-            tag = "stage%d_0" % (e + 2) if e + 2 < E else "gated%d" % e
+            tag = "stage%d_1" % (e + 2) if e + 2 < E - 1 else "gated%d" % e
             gated[e] = keep.tile([P, K], F32, name="gated%d" % e, tag=tag, align_bytes=64)
             nc.scalar.activation(gated[e][:], sums[:], COPY, scale=gate_cols[:, e : e + 1])
             turned[e] = psum.tile([P, KB, C], F32, name="turned", tag="turned")
             for kb in range(KB):
                 nc.tensor.transpose(turned[e][:, kb, :], gated[e][:, kb * P : (kb + 1) * P], identity[:])
 
-        def routed_out(e):
-            nc.scalar.copy(dx[:, :, e * C : (e + 1) * C], turned[e][:])
-
-        def shared(e):
+        def by_rows(e, m, sums):
             h, c0 = divmod(e * C, HALF)
-            sums = psum.tile([P, KB, C], F32, name="shared_sums", tag="shared_sums")
             for kb in range(KB):
                 nc.tensor.matmul_mx(
                     out=sums[:, kb, :],
-                    lhsT=codes[E][:, kb * P : (kb + 1) * P].bitcast(FP8X4),
-                    lhsT_scale=scales[E][:, kb * P : (kb + 1) * P],
+                    lhsT=codes[m][:, kb * P : (kb + 1) * P].bitcast(FP8X4),
+                    lhsT_scale=scales[m][:, kb * P : (kb + 1) * P],
                     rhs=slot_words[h][:, c0 : c0 + C].bitcast(FP8X4),
                     rhs_scale=slot_scales[h][:, c0 : c0 + C],
                     start=True,
                     stop=True,
                 )
+
+        def routed_first():
+            sums = psum.tile([P, KB, C], F32, name="first_sums", tag="first_sums", bufs=1)
+            by_rows(0, 0, sums)
+            nc.vector.tensor_tensor(dx[:, :, 0:C], sums[:], gate_wide[:].to_broadcast([P, KB, C]), MULT)
+
+        def routed_out(e):
+            nc.scalar.copy(dx[:, :, e * C : (e + 1) * C], turned[e][:])
+
+        def shared(e):
+            sums = psum.tile([P, KB, C], F32, name="shared_sums", tag="shared_sums")
+            by_rows(e, E, sums)
             nc.scalar.copy(ds[:, :, e * C : (e + 1) * C], sums[:])
 
         def scatter(e0, e1, kb):
             s0, s1 = e0 * C, e1 * C
+            if kb not in windows:
+                tag = "stage1_1" if kb == 0 else "window%d" % kb
+                windows[kb] = keep.tile([P, T], F32, name="window%d" % kb, tag=tag, align_bytes=64)
             nc.vector.tensor_tensor(windows[kb][:].indirect(list_cols(s0, s1)), dx[:, kb, s0:s1], ds[:, kb, s0:s1], ADD)
             if e1 == E:
                 nc.sync.dma_start(out[kb * P : (kb + 1) * P, :], windows[kb][:])
 
         gather_words(0)
-        gather_scales(0, "slot_scales0")
         gather_words(1)
-        for e, copy in ((0, nc.scalar.copy), (E, nc.vector.tensor_copy)):
+        gather_scales(0, "slot_scales0")
+        for e, copies in ((E, (nc.scalar.copy, nc.scalar.copy)), (0, (nc.vector.tensor_copy, nc.scalar.copy))):
             for part in range(2):
-                cast(e, part, copy)
+                cast(e, part, copies[part])
             for part in range(2):
                 quantise(e, part)
-        gather_scales(1, "stage%d_1" % E)
-        routed(0)
-        for part in range(2):
-            cast(1, part, nc.scalar.copy)
-            quantise(1, part)
+        gather_scales(1, "stage0_1")
         for e in range(E):
+            shared(e)
             if e > 0:
                 routed(e)
-            shared(e)
+            else:
+                routed_first()
+                for part in range(2):
+                    cast(1, part, nc.scalar.copy)
+                    quantise(1, part)
             if e + 2 < E:
+                cast(e + 2, 0, nc.scalar.copy)
+                quantise(e + 2, 0)
+            if e + 2 == E - 1:
                 cast(e + 2, 1, nc.scalar.copy)
-            routed_out(e)
+                quantise(e + 2, 1)
+            if e > 0:
+                routed_out(e)
             for kb in range(KB):
                 if e == E - 2 and kb == KB - 1:
                     continue
                 scatter(e - 1 if (e == E - 1 and kb == KB - 1) else e, e + 1, kb)
-            if e + 2 < E:
-                cast(e + 2, 0, nc.scalar.copy)
+            if e + 2 < E - 1:
+                cast(e + 2, 1, nc.scalar.copy)
                 quantise(e + 2, 1)
-                quantise(e + 2, 0)

from contextlib import ExitStack

import concourse.mybir as mybir
from concourse.masks import make_identity

K, T, E, C, N = 384, 1024, 8, 128, 512
FLOPS = 2 * N * K * (E * C + T)
BYTES = N * T + 16 * T + (E + 1) * N * K * 4 + T * 4 + 128 * 64 * 2 + K * T * 4

F32 = mybir.dt.float32
BF16 = mybir.dt.bfloat16
I32 = mybir.dt.int32
U32 = mybir.dt.uint32
U16 = mybir.dt.uint16
U8 = mybir.dt.uint8
FP8X4 = mybir.dt.float8_e4m3fn_x4
COPY = mybir.ActivationFunctionType.Copy
ADD = mybir.AluOpType.add
MULT = mybir.AluOpType.mult

P = 128
PACK = 4
KB = K // P
HALF = 512
LIST_COL = 16
PARTS = ((0, 256), (256, K))


def tile_moe_bds_lin_none_kernel(tc, dy_words, dy_scales, w, gate, offs, out):
    nc = tc.nc
    with ExitStack() as ctx:
        keep = ctx.enter_context(tc.tile_pool(name="keep", bufs=1))
        psum = ctx.enter_context(tc.psum_pool(name="psum", bufs=2))

        offsets = keep.tile([P, T // LIST_COL], U16, name="offsets")
        token_words = keep.tile([P, T], U32, name="token_words", align_bytes=64)
        token_scales = keep.tile([P, T], U8, name="token_scales", align_bytes=64)
        gate_rows = keep.tile([P, C], F32, name="gate_rows")
        identity = keep.tile([P, P], F32, name="identity")
        gate_cols = keep.tile([P, E], F32, name="gate_cols")

        nc.vector.memset(token_scales[:].bitcast(I32), 0)
        nc.gpsimd.memset(gate_rows[:], 0.0)
        make_identity(nc, identity[:])

        nc.sync.dma_start(offsets[:], offs)
        nc.sync.dma_start(token_words[:].bitcast(I32), dy_words[0].rearrange("p t d -> p (t d)").bitcast(I32))
        for r in range(4):
            nc.sync.dma_start(token_scales[r:P:32, :].bitcast(I32), dy_scales[0][r:16:4, :].bitcast(I32))
        nc.sync.dma_start(gate_rows[0:E, :], gate[0:1, :].rearrange("o (e c) -> (o e) c", c=C))

        order = [E] + list(range(E))
        raw = {}
        for e in order:
            raw[e] = keep.tile([P, PACK, K], F32, name="raw%d" % e)
            nc.sync.dma_start(raw[e][:], w[e].rearrange("(p j) k -> p j k", j=PACK))

        gate_t = psum.tile([P, P], F32, name="gate_t", tag="turned")
        nc.tensor.transpose(gate_t[:], gate_rows[:], identity[:])
        nc.scalar.activation(gate_cols[:], gate_t[:, 0:E], COPY)
        gate_wide = keep.tile([P, 1, C], F32, name="gate_wide", tag="stage2_1", align_bytes=64)
        gate_spread = psum.tile([P, C], F32, name="gate_spread", tag="turned")
        nc.tensor.transpose(gate_spread[:], gate_cols[:, 0:1].to_broadcast([P, P]), identity[:])
        nc.scalar.copy(gate_wide[:, 0, :], gate_spread[:])

        slot_words, slot_scales = {}, {}

        def list_cols(s0, s1):
            return offsets[:, s0 // LIST_COL : s1 // LIST_COL]

        def gather_words(h):
            slot_words[h] = keep.tile([P, HALF], U32, name="slot_words%d" % h, align_bytes=64)
            nc.vector.tensor_copy(slot_words[h][:], token_words[:].indirect(list_cols(h * HALF, (h + 1) * HALF)))

        def gather_scales(h, tag):
            slot_scales[h] = keep.tile([P, HALF], U8, name="slot_scales%d" % h, tag=tag, align_bytes=64)
            nc.vector.tensor_copy(slot_scales[h][:], token_scales[:].indirect(list_cols(h * HALF, (h + 1) * HALF)))

        grouped, codes, scales, gated, turned = {}, {}, {}, {}, {}

        def cast(e, part, copy):
            a, b = PARTS[part]
            grouped[e, part] = keep.tile(
                [P, b - a, PACK], BF16, name="grouped%d_%d" % (e, part), tag="stage%d_%d" % (e, part), align_bytes=64
            )
            copy(
                grouped[e, part][:].rearrange("p (c i) t -> p c t i", i=4),
                raw[e][:, :, a:b].rearrange("p t (c i) -> p c t i", i=4),
            )

        def quantise(e, part):
            a, b = PARTS[part]
            if e not in codes:
                codes[e] = keep.tile([P, K], U32, name="codes%d" % e, align_bytes=64)
                scales[e] = keep.tile([P, K], U8, name="scales%d" % e, align_bytes=64)
            nc.vector.quantize_mx(
                out=codes[e][:, a:b].bitcast(FP8X4),
                scales=scales[e][:, a:b],
                in_=grouped[e, part][:].rearrange("p k t -> p (k t)"),
            )

        dx = keep.tile([P, KB, T], F32, name="dx")
        ds = keep.tile([P, KB, T], F32, name="ds")
        windows = {}

        def routed(e):
            h, c0 = divmod(e * C, HALF)
            sums = psum.tile([P, K], F32, name="sums", tag="sums", bufs=1)
            for a, b in PARTS:
                nc.tensor.matmul_mx(
                    out=sums[:, a:b],
                    lhsT=slot_words[h][:, c0 : c0 + C].bitcast(FP8X4),
                    lhsT_scale=slot_scales[h][:, c0 : c0 + C],
                    rhs=codes[e][:, a:b].bitcast(FP8X4),
                    rhs_scale=scales[e][:, a:b],
                    start=True,
                    stop=True,
                )
            tag = "stage%d_1" % (e + 2) if e + 2 < E - 1 else "gated%d" % e
            gated[e] = keep.tile([P, K], F32, name="gated%d" % e, tag=tag, align_bytes=64)
            nc.scalar.activation(gated[e][:], sums[:], COPY, scale=gate_cols[:, e : e + 1])
            turned[e] = psum.tile([P, KB, C], F32, name="turned", tag="turned")
            for kb in range(KB):
                nc.tensor.transpose(turned[e][:, kb, :], gated[e][:, kb * P : (kb + 1) * P], identity[:])

        def by_rows(e, m, sums):
            h, c0 = divmod(e * C, HALF)
            for kb in range(KB):
                nc.tensor.matmul_mx(
                    out=sums[:, kb, :],
                    lhsT=codes[m][:, kb * P : (kb + 1) * P].bitcast(FP8X4),
                    lhsT_scale=scales[m][:, kb * P : (kb + 1) * P],
                    rhs=slot_words[h][:, c0 : c0 + C].bitcast(FP8X4),
                    rhs_scale=slot_scales[h][:, c0 : c0 + C],
                    start=True,
                    stop=True,
                )

        def routed_first():
            sums = psum.tile([P, KB, C], F32, name="first_sums", tag="first_sums", bufs=1)
            by_rows(0, 0, sums)
            nc.vector.tensor_tensor(dx[:, :, 0:C], sums[:], gate_wide[:].to_broadcast([P, KB, C]), MULT)

        def routed_out(e):
            nc.scalar.copy(dx[:, :, e * C : (e + 1) * C], turned[e][:])

        def shared(e):
            sums = psum.tile([P, KB, C], F32, name="shared_sums", tag="shared_sums")
            by_rows(e, E, sums)
            nc.scalar.copy(ds[:, :, e * C : (e + 1) * C], sums[:])

        def scatter(e0, e1, kb):
            s0, s1 = e0 * C, e1 * C
            if kb not in windows:
                tag = "stage1_1" if kb == 0 else "window%d" % kb
                windows[kb] = keep.tile([P, T], F32, name="window%d" % kb, tag=tag, align_bytes=64)
            nc.vector.tensor_tensor(windows[kb][:].indirect(list_cols(s0, s1)), dx[:, kb, s0:s1], ds[:, kb, s0:s1], ADD)
            if e1 == E:
                nc.sync.dma_start(out[kb * P : (kb + 1) * P, :], windows[kb][:])

        gather_words(0)
        gather_words(1)
        gather_scales(0, "slot_scales0")
        for e, copies in ((E, (nc.scalar.copy, nc.scalar.copy)), (0, (nc.vector.tensor_copy, nc.scalar.copy))):
            for part in range(2):
                cast(e, part, copies[part])
            for part in range(2):
                quantise(e, part)
        gather_scales(1, "stage0_1")
        for e in range(E):
            shared(e)
            if e > 0:
                routed(e)
            else:
                routed_first()
                for part in range(2):
                    cast(1, part, nc.scalar.copy)
                    quantise(1, part)
            if e + 2 < E:
                cast(e + 2, 0, nc.scalar.copy)
                quantise(e + 2, 0)
            if e + 2 == E - 1:
                cast(e + 2, 1, nc.scalar.copy)
                quantise(e + 2, 1)
            if e > 0:
                routed_out(e)
            for kb in range(KB):
                if e == E - 2 and kb == KB - 1:
                    continue
                scatter(e - 1 if (e == E - 1 and kb == KB - 1) else e, e + 1, kb)
            if e + 2 < E - 1:
                cast(e + 2, 1, nc.scalar.copy)
                quantise(e + 2, 1)
